import numpy as np
CORES = [6,14,22,30,38,46,54,62]
N = 8
def setup_inputs(rng):
    return {"x": rng.standard_normal((N, 128, 64), dtype=np.float32)}
def reference(x):
    s = (x.sum(axis=0, dtype=np.float64) / N).astype(x.dtype)
    b = 64 // N
    return {"y": np.stack([s[:, r * b:(r + 1) * b] for r in range(N)])}

@@ -1,0 +1,53 @@
+from concourse.bass import RemoteDMATransfer, DstId
+from concourse.mybir import AluOpType
+
+SCRATCH = {
+    "xs": ("sbuf", [128, 64], "float32"),
+    "land": ("sbuf", [128, 64], "float32"),
+    "a": ("sbuf", [128, 32], "float32"),
+    "b": ("sbuf", [128, 16], "float32"),
+    "c": ("sbuf", [128, 8], "float32"),
+    "k": ("sbuf", [128, 8], "float32"),
+    "o": ("sbuf", [128, 8], "float32"),
+}
+SEMAPHORES = ["loaded", "read", "arrived", "vec", "stored"]
+
+
+def rank_program(g, core, T, topo):
+    r = T.rank_of(core)
+    if r is None:
+        return
+    n = len(T.cores)
+    w = 8
+    S = T.sem
+    v = g.vector
+
+    g.sync.dma_start(T.xs[:], T.x[:]).then_inc(S.loaded, 16)
+
+    g.wait_ge(S.loaded, 16)
+    trs = []
+    for i in range(1, n):
+        j = (r + i) % n
+        rid, pid, _se = topo.addr(T.cores[j])
+        trs.append(RemoteDMATransfer(dst_ids=[DstId(rid=rid, pnc=pid)], dma_engine_mask=1 << (i - 1),
+                                     remote_sem=S.arrived, src=T.xs[:, j * w:(j + 1) * w],
+                                     dst=T.land[:, r * w:(r + 1) * w]))
+    g.remote_dma_fused(trs, local_sem=S.read)
+
+    v.memset(T.k[:], 0.125).then_inc(S.vec, 1)
+    v.wait_ge(S.loaded, 16)
+    v.tensor_copy(T.land[:, r * w:(r + 1) * w], T.xs[:, r * w:(r + 1) * w]).then_inc(S.vec, 1)
+    v.wait_ge(S.arrived, n - 1)
+    v.wait_ge(S.vec, 2)
+    v.tensor_tensor(T.a[:], T.land[:, 0:32], T.land[:, 32:64], AluOpType.add).then_inc(S.vec, 1)
+    v.wait_ge(S.vec, 3)
+    v.tensor_tensor(T.b[:], T.a[:, 0:16], T.a[:, 16:32], AluOpType.add).then_inc(S.vec, 1)
+    v.wait_ge(S.vec, 4)
+    v.tensor_tensor(T.c[:], T.b[:, 0:8], T.b[:, 8:16], AluOpType.add).then_inc(S.vec, 1)
+    v.wait_ge(S.vec, 5)
+    v.tensor_tensor(T.o[:], T.c[:], T.k[:], AluOpType.mult).then_inc(S.vec, 1)
+
+    g.sync.wait_ge(S.vec, 6)
+    g.sync.dma_start(T.y[:], T.o[:]).then_inc(S.stored, 16)
+    g.sync.wait_ge(S.stored, 16)
+    g.wait_ge(S.read, n - 1)

@@ -28,7 +28,7 @@ def rank_program(g, core, T, topo):
     trs = []
     for i in range(1, n):
         j = (r + i) % n
-        rid, pid, _se = topo.addr(T.cores[j])
+        rid, pid, se = topo.addr(T.cores[j])
         trs.append(RemoteDMATransfer(dst_ids=[DstId(rid=rid, pnc=pid)], dma_engine_mask=1 << (i - 1),
                                      remote_sem=S.arrived, src=T.xs[:, j * w:(j + 1) * w],
                                      dst=T.land[:, r * w:(r + 1) * w]))

from concourse.bass import RemoteDMATransfer, DstId
from concourse.mybir import AluOpType

SCRATCH = {
    "xs": ("sbuf", [128, 64], "float32"),
    "land": ("sbuf", [128, 64], "float32"),
    "a": ("sbuf", [128, 32], "float32"),
    "b": ("sbuf", [128, 16], "float32"),
    "c": ("sbuf", [128, 8], "float32"),
    "k": ("sbuf", [128, 8], "float32"),
    "o": ("sbuf", [128, 8], "float32"),
}
SEMAPHORES = ["loaded", "read", "arrived", "vec", "stored"]


def rank_program(g, core, T, topo):
    r = T.rank_of(core)
    if r is None:
        return
    n = len(T.cores)
    w = 8
    S = T.sem
    v = g.vector

    g.sync.dma_start(T.xs[:], T.x[:]).then_inc(S.loaded, 16)

    g.wait_ge(S.loaded, 16)
    trs = []
    for i in range(1, n):
        j = (r + i) % n
        rid, pid, se = topo.addr(T.cores[j])
        trs.append(RemoteDMATransfer(dst_ids=[DstId(rid=rid, pnc=pid)], dma_engine_mask=1 << (i - 1),
                                     remote_sem=S.arrived, src=T.xs[:, j * w:(j + 1) * w],
                                     dst=T.land[:, r * w:(r + 1) * w]))
    g.remote_dma_fused(trs, local_sem=S.read)

    v.memset(T.k[:], 0.125).then_inc(S.vec, 1)
    v.wait_ge(S.loaded, 16)
    v.tensor_copy(T.land[:, r * w:(r + 1) * w], T.xs[:, r * w:(r + 1) * w]).then_inc(S.vec, 1)
    v.wait_ge(S.arrived, n - 1)
    v.wait_ge(S.vec, 2)
    v.tensor_tensor(T.a[:], T.land[:, 0:32], T.land[:, 32:64], AluOpType.add).then_inc(S.vec, 1)
    v.wait_ge(S.vec, 3)
    v.tensor_tensor(T.b[:], T.a[:, 0:16], T.a[:, 16:32], AluOpType.add).then_inc(S.vec, 1)
    v.wait_ge(S.vec, 4)
    v.tensor_tensor(T.c[:], T.b[:, 0:8], T.b[:, 8:16], AluOpType.add).then_inc(S.vec, 1)
    v.wait_ge(S.vec, 5)
    v.tensor_tensor(T.o[:], T.c[:], T.k[:], AluOpType.mult).then_inc(S.vec, 1)

    g.sync.wait_ge(S.vec, 6)
    g.sync.dma_start(T.y[:], T.o[:]).then_inc(S.stored, 16)
    g.sync.wait_ge(S.stored, 16)
    g.wait_ge(S.read, n - 1)
